import numpy as np
import ml_dtypes


def mxq(x, axis, fmt="e4m3"):
    dtype, down = {"e4m3": (ml_dtypes.float8_e4m3fn, 7), "e5m2": (ml_dtypes.float8_e5m2, 14)}[fmt]
    v = np.moveaxis(np.asarray(x, np.float32).astype(ml_dtypes.bfloat16).astype(np.float64), axis, -1)
    blocks = v.reshape(v.shape[:-1] + (-1, 32))
    amax = np.abs(blocks).max(-1, keepdims=True)
    byte = np.maximum(np.where(amax > 0, np.frexp(amax)[1] - 1 + 127, 0) - down, 1)
    scale = np.exp2(byte - 127.0)
    codes = (blocks / scale).astype(np.float32).astype(dtype).astype(np.float64)
    return np.moveaxis((codes * scale).reshape(v.shape), -1, axis)


WIDE = False


def mx_kscale(k):
    if not WIDE:
        return np.ones(k)
    levels = np.array([10, -10, 5, -5, 0])
    if k % 512:
        return np.exp2(np.random.permutation(np.resize(levels, k // 32))).repeat(32)
    a = np.empty((k // 512, 16))
    for p in range(k // 512):
        a[p, :8] = np.random.permutation(np.resize(levels, 8))
        for g in range(8):
            far = levels[np.abs(levels - a[p, g]) >= 10]
            a[p, g + 8] = far[np.random.randint(len(far))]
    return np.exp2(a.ravel()).repeat(32)


def f64(x):
    return np.asarray(x).astype(np.float64)


E2M1 = np.array([0.0, 0.5, 1.0, 1.5, 2.0, 3.0, 4.0, 6.0, -0.0, -0.5, -1.0, -1.5, -2.0, -3.0, -4.0, -6.0])


def pack_weight(w, fmt):
    k, n = w.shape
    w = f64(np.asarray(w, np.float32).astype(ml_dtypes.bfloat16)).reshape(k // 32, 32, n)
    amax = np.abs(w).max(1)
    if fmt == "e4m3":
        byte = np.frexp(amax)[1] - 1 + 127 - 7
    else:
        mant, ex = np.frexp(amax / 6.0)
        byte = np.where(mant > 0.5, ex, ex - 1) + 127
    byte = np.clip(np.where(amax > 0, byte, 1), 1, 254)
    scaled = (w * np.exp2(127.0 - byte)[:, None, :]).reshape(k, n).astype(np.float32)
    by_word = np.ascontiguousarray(scaled.reshape(k // 512, 128, 4, n).transpose(0, 1, 3, 2))
    if fmt == "e4m3":
        words = by_word.astype(ml_dtypes.float8_e4m3fn).view(np.uint8)
    else:
        c = by_word.astype(ml_dtypes.float4_e2m1fn).view(np.uint8) & 0xF
        words = (c[..., 0::2] | (c[..., 1::2] << 4)).reshape(k // 512, 128, 2 * n)
    return np.ascontiguousarray(words), np.ascontiguousarray(byte.astype(np.uint8).reshape(k // 512, 16, n))


def unpack_weight(words, scales, fmt):
    g, _, n = scales.shape
    words = np.ascontiguousarray(words).reshape(g, 128, n, -1)
    if fmt == "e4m3":
        vals = words.view(ml_dtypes.float8_e4m3fn).astype(np.float64)
    else:
        nib = np.empty((g, 128, n, 4), np.uint8)
        nib[..., 0::2] = words & 0xF
        nib[..., 1::2] = words >> 4
        vals = E2M1[nib]
    vals = vals * np.repeat(np.exp2(scales.astype(np.float64) - 127.0), 8, axis=1)[..., None]
    return vals.transpose(0, 1, 3, 2).reshape(g * 512, n)


K, M, T = 512, 1536, 1536


def setup_inputs():
    n = np.random.standard_normal
    s = mx_kscale(K)[:, None]
    p_w4 = pack_weight(n((K, M)) / np.sqrt(K) / s, "e2m1")
    p_w8 = pack_weight(n((K, M)) / np.sqrt(K) / s, "e4m3")
    return {
        "x": (n((K, T)) * s).astype(np.float32),
        "w4_words": p_w4[0],
        "w4_scales": p_w4[1],
        "w8_words": p_w8[0],
        "w8_scales": p_w8[1],
    }


def reference(x, w4_words, w4_scales, w8_words, w8_scales):
    xa_, xb_ = mxq(np.maximum(f64(x), 0.0), 0, "e4m3"), mxq(np.maximum(-f64(x), 0.0), 0, "e4m3")
    w4_ = unpack_weight(w4_words, w4_scales, "e2m1")
    w8_ = unpack_weight(w8_words, w8_scales, "e4m3")
    y = xa_.T @ w4_ + xb_.T @ w8_
    return y

@@ -1,0 +1,140 @@
+from contextlib import ExitStack
+
+import concourse.mybir as mybir
+
+K, M, T = 512, 1536, 1536
+FLOPS = 2 * 2 * K * M * T
+
+F32 = mybir.dt.float32
+BF16 = mybir.dt.bfloat16
+I32 = mybir.dt.int32
+U32 = mybir.dt.uint32
+U8 = mybir.dt.uint8
+FP8X4 = mybir.dt.float8_e4m3fn_x4
+FP4X4 = mybir.dt.float4_e2m1fn_x4
+ALU = mybir.AluOpType
+
+P = 128
+PACK = 4
+T_TILE = 128
+N_TILE = 512
+BANKS = M // N_TILE
+UNIT = 256
+X_CHUNKS = (256, 512, 768)
+W8_ROW = 4
+
+
+def tile_mix_feat_tm_crelu_none_kernel(tc, x, w4_words, w4_scales, w8_words, w8_scales, out):
+    nc = tc.nc
+    with ExitStack() as ctx:
+        keep = ctx.enter_context(tc.tile_pool(name="keep", bufs=1))
+        psum = ctx.enter_context(tc.psum_pool(name="psum", bufs=8))
+        ctx.enter_context(tc.manual_schedule())
+
+        w4 = keep.tile([P, 2 * M], U8, align_bytes=64)
+        w8 = keep.tile([P, M], U32, align_bytes=64)
+        s4 = keep.tile([P, M], U8, align_bytes=64)
+        s8 = keep.tile([P, M], U8, align_bytes=64)
+        nc.vector.memset(s4[:].bitcast(I32), 0)
+        nc.vector.memset(s8[:].bitcast(I32), 0)
+
+        x_rows = x.rearrange("(p j) t -> p j t", j=PACK)
+        starts = [sum(X_CHUNKS[:c]) for c in range(len(X_CHUNKS))]
+        raw = [keep.tile([P, PACK, w], F32, name="raw%d" % c) for c, w in enumerate(X_CHUNKS)]
+
+        def load_x(c):
+            nc.sync.dma_start(out=raw[c][:], in_=x_rows[:, :, starts[c] : starts[c] + X_CHUNKS[c]])
+
+        def load_scales(plane, rows, first):
+            for r in range(4):
+                nc.sync.dma_start(
+                    out=plane[:].bitcast(I32)[first + r : P : 32, :],
+                    in_=rows[0].bitcast(I32)[r:16:4, :],
+                )
+
+        load_x(0)
+        nc.sync.dma_start(out=w4[:].bitcast(I32), in_=w4_words[0].bitcast(I32))
+        load_scales(s4, w4_scales, 0)
+        nc.sync.dma_start(out=w8[:].bitcast(I32), in_=w8_words[0].rearrange("p n i -> p (n i)").bitcast(I32))
+        load_x(1)
+        load_scales(s8, w8_scales, W8_ROW)
+        load_x(2)
+
+        codes = {}
+
+        def quantise(u):
+            t0 = u * UNIT
+            c = max(i for i in range(len(starts)) if starts[i] <= t0)
+            src = raw[c][:, :, t0 - starts[c] : t0 - starts[c] + UNIT].rearrange("p j t -> p t j")
+            pos = keep.tile([P, UNIT, PACK], BF16, name="pos%d" % u, align_bytes=64)
+            neg = keep.tile([P, UNIT, PACK], BF16, name="neg%d" % u, align_bytes=64)
+            nc.vector.tensor_scalar(out=pos[:], in0=src, scalar1=0.0, scalar2=None, op0=ALU.max)
+            nc.vector.tensor_scalar(out=neg[:], in0=src, scalar1=-1.0, scalar2=0.0, op0=ALU.mult, op1=ALU.max)
+            for side, part in (("a", pos), ("b", neg)):
+                words = keep.tile([P, UNIT], U32, name="codes_%s%d" % (side, u), align_bytes=64)
+                scales = keep.tile([P, UNIT], U8, name="scales_%s%d" % (side, u), align_bytes=64)
+                nc.vector.quantize_mx(
+                    out=words[:].bitcast(FP8X4), scales=scales[:], in_=part[:].rearrange("p t j -> p (t j)")
+                )
+                codes[side, u] = (words, scales)
+
+        acc = {}
+
+        def pass_a(i):
+            u, off = divmod(i * T_TILE, UNIT)
+            words, scales = codes["a", u]
+            for b in range(BANKS):
+                acc[i, b] = psum.tile([T_TILE, N_TILE], F32, name="acc")
+                nc.tensor.matmul_mx(
+                    out=acc[i, b][:],
+                    lhsT=words[:, off : off + T_TILE].bitcast(FP8X4),
+                    lhsT_scale=scales[:, off : off + T_TILE],
+                    rhs=w4[:, 2 * b * N_TILE : 2 * (b + 1) * N_TILE].bitcast(FP4X4),
+                    rhs_scale=s4[:, b * N_TILE : (b + 1) * N_TILE],
+                    start=True,
+                    stop=False,
+                )
+
+        def pass_b(i):
+            u, off = divmod(i * T_TILE, UNIT)
+            words, scales = codes["b", u]
+            for b in range(BANKS):
+                nc.tensor.matmul_mx(
+                    out=acc[i, b][:],
+                    lhsT=words[:, off : off + T_TILE].bitcast(FP8X4),
+                    lhsT_scale=scales[:, off : off + T_TILE],
+                    rhs=w8[:, b * N_TILE : (b + 1) * N_TILE].bitcast(FP8X4),
+                    rhs_scale=s8[W8_ROW:P, b * N_TILE : (b + 1) * N_TILE],
+                    start=False,
+                    stop=True,
+                )
+
+        def store(i, vector_banks):
+            result = keep.tile([T_TILE, M], F32, name="result%d" % i)
+            for b in range(BANKS):
+                cols = result[:, b * N_TILE : (b + 1) * N_TILE]
+                if b >= BANKS - vector_banks:
+                    nc.vector.tensor_copy(out=cols, in_=acc[i, b][:])
+                else:
+                    nc.scalar.copy(out=cols, in_=acc[i, b][:])
+            nc.sync.dma_start(out=out[i * T_TILE : (i + 1) * T_TILE, :], in_=result[:])
+
+        units = T // UNIT
+        quantise(0)
+        quantise(1)
+        pass_a(0)
+        pass_a(1)
+        pass_b(0)
+        pass_b(1)
+        for u in range(units):
+            left = u + 2 < units
+            if u > 0:
+                pass_a(2 * u)
+                pass_b(2 * u)
+            if left:
+                quantise(u + 2)
+            store(2 * u, 0 if left else 1)
+            if u > 0:
+                pass_a(2 * u + 1)
+                pass_b(2 * u + 1)
+            store(2 * u + 1, 1 if left else 2)

@@ -20,7 +20,7 @@ T_TILE = 128
 N_TILE = 512
 BANKS = M // N_TILE
 UNIT = 256
-X_CHUNKS = (256, 512, 768)
+X_CHUNKS = (256, 256, 512, 512)
 W8_ROW = 4
 
 
@@ -45,20 +45,20 @@ def tile_mix_feat_tm_crelu_none_kernel(tc, x, w4_words, w4_scales, w8_words, w8_
         def load_x(c):
             nc.sync.dma_start(out=raw[c][:], in_=x_rows[:, :, starts[c] : starts[c] + X_CHUNKS[c]])
 
-        def load_scales(plane, rows, first):
+        def load_scales(queue, plane, rows, first):
             for r in range(4):
-                nc.sync.dma_start(
+                queue.dma_start(
                     out=plane[:].bitcast(I32)[first + r : P : 32, :],
                     in_=rows[0].bitcast(I32)[r:16:4, :],
                 )
 
         load_x(0)
+        load_scales(nc.sync, s4, w4_scales, 0)
         nc.sync.dma_start(out=w4[:].bitcast(I32), in_=w4_words[0].bitcast(I32))
-        load_scales(s4, w4_scales, 0)
         nc.sync.dma_start(out=w8[:].bitcast(I32), in_=w8_words[0].rearrange("p n i -> p (n i)").bitcast(I32))
-        load_x(1)
-        load_scales(s8, w8_scales, W8_ROW)
-        load_x(2)
+        load_scales(nc.sync, s8, w8_scales, W8_ROW)
+        for c in range(1, len(X_CHUNKS)):
+            load_x(c)
 
         codes = {}
 
@@ -68,15 +68,22 @@ def tile_mix_feat_tm_crelu_none_kernel(tc, x, w4_words, w4_scales, w8_words, w8_
             src = raw[c][:, :, t0 - starts[c] : t0 - starts[c] + UNIT].rearrange("p j t -> p t j")
             pos = keep.tile([P, UNIT, PACK], BF16, name="pos%d" % u, align_bytes=64)
             neg = keep.tile([P, UNIT, PACK], BF16, name="neg%d" % u, align_bytes=64)
-            nc.vector.tensor_scalar(out=pos[:], in0=src, scalar1=0.0, scalar2=None, op0=ALU.max)
-            nc.vector.tensor_scalar(out=neg[:], in0=src, scalar1=-1.0, scalar2=0.0, op0=ALU.mult, op1=ALU.max)
-            for side, part in (("a", pos), ("b", neg)):
+
+            def to_mx(side, part):
                 words = keep.tile([P, UNIT], U32, name="codes_%s%d" % (side, u), align_bytes=64)
                 scales = keep.tile([P, UNIT], U8, name="scales_%s%d" % (side, u), align_bytes=64)
                 nc.vector.quantize_mx(
                     out=words[:].bitcast(FP8X4), scales=scales[:], in_=part[:].rearrange("p t j -> p (t j)")
                 )
                 codes[side, u] = (words, scales)
+
+            nc.vector.tensor_scalar(out=pos[:], in0=src, scalar1=0.0, scalar2=None, op0=ALU.max)
+            if u == 0:
+                to_mx("a", pos)
+            nc.vector.tensor_scalar(out=neg[:], in0=src, scalar1=-1.0, scalar2=0.0, op0=ALU.mult, op1=ALU.max)
+            if u > 0:
+                to_mx("a", pos)
+            to_mx("b", neg)
 
         acc = {}
 
@@ -109,32 +116,30 @@ def tile_mix_feat_tm_crelu_none_kernel(tc, x, w4_words, w4_scales, w8_words, w8_
                     stop=True,
                 )
 
-        def store(i, vector_banks):
+        def store(i, vector_banks, pieces=1):
+            width = M // pieces
+            rows = slice(i * T_TILE, (i + 1) * T_TILE)
             result = keep.tile([T_TILE, M], F32, name="result%d" % i)
             for b in range(BANKS):
                 cols = result[:, b * N_TILE : (b + 1) * N_TILE]
-                if b >= BANKS - vector_banks:
+                if b in vector_banks:
                     nc.vector.tensor_copy(out=cols, in_=acc[i, b][:])
                 else:
                     nc.scalar.copy(out=cols, in_=acc[i, b][:])
-            nc.sync.dma_start(out=out[i * T_TILE : (i + 1) * T_TILE, :], in_=result[:])
+                end = (b + 1) * N_TILE
+                if end % width == 0:
+                    nc.sync.dma_start(out=out[rows, end - width : end], in_=result[:, end - width : end])
 
         units = T // UNIT
         quantise(0)
         quantise(1)
-        pass_a(0)
-        pass_a(1)
-        pass_b(0)
-        pass_b(1)
         for u in range(units):
             left = u + 2 < units
-            if u > 0:
-                pass_a(2 * u)
-                pass_b(2 * u)
+            pass_a(2 * u)
+            pass_b(2 * u)
             if left:
                 quantise(u + 2)
-            store(2 * u, 0 if left else 1)
-            if u > 0:
-                pass_a(2 * u + 1)
-                pass_b(2 * u + 1)
-            store(2 * u + 1, 1 if left else 2)
+            store(2 * u, () if left else (1,))
+            pass_a(2 * u + 1)
+            pass_b(2 * u + 1)
+            store(2 * u + 1, (2,) if left else (0, 2), BANKS if u == units - 1 else 1)

@@ -20,7 +20,7 @@ T_TILE = 128
 N_TILE = 512
 BANKS = M // N_TILE
 UNIT = 256
-X_CHUNKS = (256, 256, 512, 512)
+X_CHUNKS = (512, 1024)
 W8_ROW = 4
 
 
@@ -78,10 +78,10 @@ def tile_mix_feat_tm_crelu_none_kernel(tc, x, w4_words, w4_scales, w8_words, w8_
                 codes[side, u] = (words, scales)
 
             nc.vector.tensor_scalar(out=pos[:], in0=src, scalar1=0.0, scalar2=None, op0=ALU.max)
-            if u == 0:
+            if t0 in starts:
                 to_mx("a", pos)
             nc.vector.tensor_scalar(out=neg[:], in0=src, scalar1=-1.0, scalar2=0.0, op0=ALU.mult, op1=ALU.max)
-            if u > 0:
+            if t0 not in starts:
                 to_mx("a", pos)
             to_mx("b", neg)
 
@@ -132,14 +132,13 @@ def tile_mix_feat_tm_crelu_none_kernel(tc, x, w4_words, w4_scales, w8_words, w8_
 
         units = T // UNIT
         quantise(0)
-        quantise(1)
         for u in range(units):
-            left = u + 2 < units
+            left = u + 1 < units
             pass_a(2 * u)
             pass_b(2 * u)
             if left:
-                quantise(u + 2)
+                quantise(u + 1)
             store(2 * u, () if left else (1,))
             pass_a(2 * u + 1)
             pass_b(2 * u + 1)
-            store(2 * u + 1, (2,) if left else (0, 2), BANKS if u == units - 1 else 1)
+            store(2 * u + 1, (2,) if left else (0, 2))

@@ -19,7 +19,7 @@ PACK = 4
 T_TILE = 128
 N_TILE = 512
 BANKS = M // N_TILE
-UNIT = 256
+UNIT = 128
 X_CHUNKS = (512, 1024)
 W8_ROW = 4
 
@@ -78,11 +78,8 @@ def tile_mix_feat_tm_crelu_none_kernel(tc, x, w4_words, w4_scales, w8_words, w8_
                 codes[side, u] = (words, scales)
 
             nc.vector.tensor_scalar(out=pos[:], in0=src, scalar1=0.0, scalar2=None, op0=ALU.max)
-            if t0 in starts:
-                to_mx("a", pos)
             nc.vector.tensor_scalar(out=neg[:], in0=src, scalar1=-1.0, scalar2=0.0, op0=ALU.mult, op1=ALU.max)
-            if t0 not in starts:
-                to_mx("a", pos)
+            to_mx("a", pos)
             to_mx("b", neg)
 
         acc = {}
@@ -116,29 +113,29 @@ def tile_mix_feat_tm_crelu_none_kernel(tc, x, w4_words, w4_scales, w8_words, w8_
                     stop=True,
                 )
 
-        def store(i, vector_banks, pieces=1):
-            width = M // pieces
+        def store(i, vector_banks, ends):
             rows = slice(i * T_TILE, (i + 1) * T_TILE)
             result = keep.tile([T_TILE, M], F32, name="result%d" % i)
+            begin = 0
             for b in range(BANKS):
-                cols = result[:, b * N_TILE : (b + 1) * N_TILE]
+                end = (b + 1) * N_TILE
+                cols = result[:, b * N_TILE : end]
                 if b in vector_banks:
                     nc.vector.tensor_copy(out=cols, in_=acc[i, b][:])
                 else:
                     nc.scalar.copy(out=cols, in_=acc[i, b][:])
-                end = (b + 1) * N_TILE
-                if end % width == 0:
-                    nc.sync.dma_start(out=out[rows, end - width : end], in_=result[:, end - width : end])
+                if end in ends:
+                    nc.sync.dma_start(out=out[rows, begin:end], in_=result[:, begin:end])
+                    begin = end
 
-        units = T // UNIT
+        tiles = T // T_TILE
         quantise(0)
-        for u in range(units):
-            left = u + 1 < units
-            pass_a(2 * u)
-            pass_b(2 * u)
-            if left:
-                quantise(u + 1)
-            store(2 * u, () if left else (1,))
-            pass_a(2 * u + 1)
-            pass_b(2 * u + 1)
-            store(2 * u + 1, (2,) if left else (0, 2))
+        quantise(1)
+        for i in range(tiles):
+            pass_a(i)
+            pass_b(i)
+            if i + 2 < tiles:
+                quantise(i + 2)
+                store(i, (2,) if i % 2 else (), (M,))
+            else:
+                store(i, (0, 2) if i % 2 else (1,), (M - N_TILE, M) if i == tiles - 1 else (M,))

from contextlib import ExitStack

import concourse.mybir as mybir

K, M, T = 512, 1536, 1536
FLOPS = 2 * 2 * K * M * T

F32 = mybir.dt.float32
BF16 = mybir.dt.bfloat16
I32 = mybir.dt.int32
U32 = mybir.dt.uint32
U8 = mybir.dt.uint8
FP8X4 = mybir.dt.float8_e4m3fn_x4
FP4X4 = mybir.dt.float4_e2m1fn_x4
ALU = mybir.AluOpType

P = 128
PACK = 4
T_TILE = 128
N_TILE = 512
BANKS = M // N_TILE
UNIT = 128
X_CHUNKS = (512, 1024)
W8_ROW = 4


def tile_mix_feat_tm_crelu_none_kernel(tc, x, w4_words, w4_scales, w8_words, w8_scales, out):
    nc = tc.nc
    with ExitStack() as ctx:
        keep = ctx.enter_context(tc.tile_pool(name="keep", bufs=1))
        psum = ctx.enter_context(tc.psum_pool(name="psum", bufs=8))
        ctx.enter_context(tc.manual_schedule())

        w4 = keep.tile([P, 2 * M], U8, align_bytes=64)
        w8 = keep.tile([P, M], U32, align_bytes=64)
        s4 = keep.tile([P, M], U8, align_bytes=64)
        s8 = keep.tile([P, M], U8, align_bytes=64)
        nc.vector.memset(s4[:].bitcast(I32), 0)
        nc.vector.memset(s8[:].bitcast(I32), 0)

        x_rows = x.rearrange("(p j) t -> p j t", j=PACK)
        starts = [sum(X_CHUNKS[:c]) for c in range(len(X_CHUNKS))]
        raw = [keep.tile([P, PACK, w], F32, name="raw%d" % c) for c, w in enumerate(X_CHUNKS)]

        def load_x(c):
            nc.sync.dma_start(out=raw[c][:], in_=x_rows[:, :, starts[c] : starts[c] + X_CHUNKS[c]])

        def load_scales(queue, plane, rows, first):
            for r in range(4):
                queue.dma_start(
                    out=plane[:].bitcast(I32)[first + r : P : 32, :],
                    in_=rows[0].bitcast(I32)[r:16:4, :],
                )

        load_x(0)
        load_scales(nc.sync, s4, w4_scales, 0)
        nc.sync.dma_start(out=w4[:].bitcast(I32), in_=w4_words[0].bitcast(I32))
        nc.sync.dma_start(out=w8[:].bitcast(I32), in_=w8_words[0].rearrange("p n i -> p (n i)").bitcast(I32))
        load_scales(nc.sync, s8, w8_scales, W8_ROW)
        for c in range(1, len(X_CHUNKS)):
            load_x(c)

        codes = {}

        def quantise(u):
            t0 = u * UNIT
            c = max(i for i in range(len(starts)) if starts[i] <= t0)
            src = raw[c][:, :, t0 - starts[c] : t0 - starts[c] + UNIT].rearrange("p j t -> p t j")
            pos = keep.tile([P, UNIT, PACK], BF16, name="pos%d" % u, align_bytes=64)
            neg = keep.tile([P, UNIT, PACK], BF16, name="neg%d" % u, align_bytes=64)

            def to_mx(side, part):
                words = keep.tile([P, UNIT], U32, name="codes_%s%d" % (side, u), align_bytes=64)
                scales = keep.tile([P, UNIT], U8, name="scales_%s%d" % (side, u), align_bytes=64)
                nc.vector.quantize_mx(
                    out=words[:].bitcast(FP8X4), scales=scales[:], in_=part[:].rearrange("p t j -> p (t j)")
                )
                codes[side, u] = (words, scales)

            nc.vector.tensor_scalar(out=pos[:], in0=src, scalar1=0.0, scalar2=None, op0=ALU.max)
            nc.vector.tensor_scalar(out=neg[:], in0=src, scalar1=-1.0, scalar2=0.0, op0=ALU.mult, op1=ALU.max)
            to_mx("a", pos)
            to_mx("b", neg)

        acc = {}

        def pass_a(i):
            u, off = divmod(i * T_TILE, UNIT)
            words, scales = codes["a", u]
            for b in range(BANKS):
                acc[i, b] = psum.tile([T_TILE, N_TILE], F32, name="acc")
                nc.tensor.matmul_mx(
                    out=acc[i, b][:],
                    lhsT=words[:, off : off + T_TILE].bitcast(FP8X4),
                    lhsT_scale=scales[:, off : off + T_TILE],
                    rhs=w4[:, 2 * b * N_TILE : 2 * (b + 1) * N_TILE].bitcast(FP4X4),
                    rhs_scale=s4[:, b * N_TILE : (b + 1) * N_TILE],
                    start=True,
                    stop=False,
                )

        def pass_b(i):
            u, off = divmod(i * T_TILE, UNIT)
            words, scales = codes["b", u]
            for b in range(BANKS):
                nc.tensor.matmul_mx(
                    out=acc[i, b][:],
                    lhsT=words[:, off : off + T_TILE].bitcast(FP8X4),
                    lhsT_scale=scales[:, off : off + T_TILE],
                    rhs=w8[:, b * N_TILE : (b + 1) * N_TILE].bitcast(FP8X4),
                    rhs_scale=s8[W8_ROW:P, b * N_TILE : (b + 1) * N_TILE],
                    start=False,
                    stop=True,
                )

        def store(i, vector_banks, ends):
            rows = slice(i * T_TILE, (i + 1) * T_TILE)
            result = keep.tile([T_TILE, M], F32, name="result%d" % i)
            begin = 0
            for b in range(BANKS):
                end = (b + 1) * N_TILE
                cols = result[:, b * N_TILE : end]
                if b in vector_banks:
                    nc.vector.tensor_copy(out=cols, in_=acc[i, b][:])
                else:
                    nc.scalar.copy(out=cols, in_=acc[i, b][:])
                if end in ends:
                    nc.sync.dma_start(out=out[rows, begin:end], in_=result[:, begin:end])
                    begin = end

        tiles = T // T_TILE
        quantise(0)
        quantise(1)
        for i in range(tiles):
            pass_a(i)
            pass_b(i)
            if i + 2 < tiles:
                quantise(i + 2)
                store(i, (2,) if i % 2 else (), (M,))
            else:
                store(i, (0, 2) if i % 2 else (1,), (M - N_TILE, M) if i == tiles - 1 else (M,))
